import numpy as np
import ml_dtypes


def mxq(x, axis, fmt="e4m3"):
    dtype, down = {"e4m3": (ml_dtypes.float8_e4m3fn, 7), "e5m2": (ml_dtypes.float8_e5m2, 14)}[fmt]
    v = np.moveaxis(np.asarray(x, np.float32).astype(ml_dtypes.bfloat16).astype(np.float64), axis, -1)
    blocks = v.reshape(v.shape[:-1] + (-1, 32))
    amax = np.abs(blocks).max(-1, keepdims=True)
    byte = np.maximum(np.where(amax > 0, np.frexp(amax)[1] - 1 + 127, 0) - down, 1)
    scale = np.exp2(byte - 127.0)
    codes = (blocks / scale).astype(np.float32).astype(dtype).astype(np.float64)
    return np.moveaxis((codes * scale).reshape(v.shape), -1, axis)


WIDE = False


def mx_kscale(k):
    if not WIDE:
        return np.ones(k)
    levels = np.array([24, -24, 12, -12, 0])
    if k % 512:
        return np.exp2(np.random.permutation(np.resize(levels, k // 32))).repeat(32)
    a = np.empty((k // 512, 16))
    for p in range(k // 512):
        a[p, :8] = np.random.permutation(np.resize(levels, 8))
        for g in range(8):
            far = levels[np.abs(levels - a[p, g]) >= 10]
            a[p, g + 8] = far[np.random.randint(len(far))]
    return np.exp2(a.ravel()).repeat(32)


def f64(x):
    return np.asarray(x).astype(np.float64)


def striped8(idx):
    return np.concatenate([v.reshape(-1, 16).T for v in idx]).astype(np.uint16)


def unstriped8(offs):
    return np.stack([offs[16 * g:16 * g + 16].T.reshape(-1) for g in range(8)]).astype(np.int64)


def planes(y):
    n, m = y.shape
    v = y.astype(np.float32).astype(ml_dtypes.bfloat16).astype(np.float64).reshape(n // 32, 32, m)
    top = np.abs(v).max(1)
    byte = np.clip(np.where(top > 0, np.frexp(top)[1] - 1 + 127 - 7, 1), 1, 254)
    codes = (v * np.exp2(127.0 - byte)[:, None, :]).reshape(n, m).astype(np.float32).astype(ml_dtypes.float8_e4m3fn).view(np.uint8)
    words = codes.reshape(n // 512, 128, 4, m).transpose(0, 1, 3, 2)
    return np.ascontiguousarray(words), np.ascontiguousarray(byte.astype(np.uint8).reshape(n // 512, 16, m))


def silu(f):
    return f / (1.0 + np.exp(-np.maximum(f, -700.0)))


K, N, T, J = 512, 512, 2048, 1024


def setup_inputs():
    n = np.random.standard_normal
    s = mx_kscale(K)[:, None]
    return {
        "xT": (n((K, T)) * s).astype(np.float32),
        "wgt": np.repeat(np.random.uniform(0.5, 2.0, (8, J)), 16, axis=0).astype(np.float32),
        "wk": (n((K, N)) / np.sqrt(K) / s).astype(np.float32),
        "wv": (n((K, N)) / np.sqrt(K) / s).astype(np.float32),
        "st": (n((N, J))).astype(np.float32),
        "offs": striped8(np.stack([np.random.permutation(T)[:J] for _ in range(8)])),
    }


def reference(xT, wgt, wk, wv, st, offs):
    idx = unstriped8(offs)
    rows = np.arange(K)
    xg = f64(wgt)[rows // 4 % 128] * f64(xT)[rows[:, None], idx[rows % 512 // 64]]
    xT_ = mxq(xg, 0, "e4m3")
    wk_ = mxq(f64(wk), 0, "e4m3")
    wv_ = mxq(f64(wv), 0, "e4m3")
    ke = wk_.T @ xT_
    ve = wv_.T @ xT_
    gate = silu(ke * f64(st))
    out_0 = gate * ve
    return (out_0,) + planes(out_0)

@@ -1,0 +1,224 @@
+from contextlib import ExitStack
+
+import concourse.mybir as mybir
+
+K, N, T, J = 512, 512, 2048, 1024
+FLOPS = 2 * 2 * K * N * J
+
+F32 = mybir.dt.float32
+BF16 = mybir.dt.bfloat16
+I32 = mybir.dt.int32
+U32 = mybir.dt.uint32
+U16 = mybir.dt.uint16
+U8 = mybir.dt.uint8
+FP8X4 = mybir.dt.float8_e4m3fn_x4
+MULT = mybir.AluOpType.mult
+ADD = mybir.AluOpType.add
+SILU = mybir.ActivationFunctionType.Silu
+
+P = 128
+PACK = 4
+BANK = 512
+X_CHUNKS = (256, 256, 256, 256)
+CHUNKS = (256, 256, 256, 128, 128)
+ST_PIECES = ((0, 2, 0, 256), (2, 4, 0, 256), (0, 4, 256, 512), (0, 4, 512, 768), (0, 4, 768, 1024))
+
+
+def tile_list_siluP_kernel(tc, xT, wgt, wk, wv, st, offs, out_0, out_1, out_2):
+    nc = tc.nc
+    with ExitStack() as ctx:
+        keep = ctx.enter_context(tc.tile_pool(name="keep", bufs=1))
+        psum = ctx.enter_context(tc.psum_pool(name="psum", bufs=4))
+
+        starts = [sum(CHUNKS[:c]) for c in range(len(CHUNKS))]
+        x_starts = [sum(X_CHUNKS[:c]) for c in range(len(X_CHUNKS))]
+        units = []
+        for c, w in enumerate(CHUNKS):
+            rows = BANK // w
+            for t0 in range(0, PACK, rows):
+                units.append((c, t0, rows))
+
+        warm = keep.tile([P, 8], F32, name="warm")
+        nc.vector.memset(warm[:, 0:4], 0.0)
+        nc.scalar.activation(warm[:, 4:8], warm[:, 0:4], SILU)
+
+        offsets = keep.tile([P, J // 16], U16, name="offsets")
+        nc.sync.dma_start(offsets[:], offs)
+        wgt_sb = keep.tile([P, J], F32, name="wgt_sb")
+        nc.sync.dma_start(wgt_sb[:], wgt)
+        x_rows = xT.rearrange("(p i) t -> i p t", i=PACK)
+        x_sb = []
+
+        def load_x(i):
+            plane = keep.tile([P, T], F32, name=f"x{i}")
+            nc.sync.dma_start(plane[:], x_rows[i])
+            x_sb.append(plane)
+
+        st_rows = st.rearrange("(p i) j -> p i j", i=PACK)
+        y_rows = out_0.rearrange("(p i) j -> p i j", i=PACK)
+        st_sb = []
+
+        def load_w(name, w):
+            raw = keep.tile([P, PACK, N], F32, name=name, tag=name, align_bytes=64)
+            nc.sync.dma_start(raw[:], w.rearrange("(p i) n -> p i n", i=PACK))
+            return raw
+
+        def load_st(s):
+            t0, t1, j0, j1 = ST_PIECES[s]
+            piece = keep.tile([P, t1 - t0, j1 - j0], F32, name=f"st{s}")
+            nc.sync.dma_start(piece[:], st_rows[:, t0:t1, j0:j1])
+            st_sb.append(piece)
+
+        def st_of(u):
+            c, t0, rows = units[u]
+            j0, w = starts[c], CHUNKS[c]
+            for s, (a, b, lo, hi) in enumerate(ST_PIECES):
+                if a <= t0 and t0 + rows <= b and lo <= j0 and j0 + w <= hi:
+                    return st_sb[s][:, t0 - a : t0 - a + rows, j0 - lo : j0 - lo + w]
+
+        load_x(0)
+        load_x(1)
+        wk_raw = load_w("wk_raw", wk)
+        load_x(2)
+        load_x(3)
+        for s in range(0):
+            load_st(s)
+        wv_raw = load_w("wv_raw", wv)
+        for s in range(0, len(ST_PIECES)):
+            load_st(s)
+
+        g01 = keep.tile([P, 2, J], F32, name="g01")
+        for i in range(2):
+            nc.vector.tensor_tensor(g01[:, i, :], x_sb[i][:].indirect(offsets[:]), wgt_sb[:], MULT)
+        def round_w(name, raw, v_end, g_end):
+            wb = keep.tile([P, PACK, P, PACK], BF16, name=name, align_bytes=64)
+            dst = wb[:].rearrange("p t m i -> p m i t")
+            src = raw[:].rearrange("p i (m t) -> p m i t", t=PACK)
+            if v_end > 0:
+                nc.vector.tensor_copy(dst[:, 0:v_end], src[:, 0:v_end])
+            if g_end > v_end:
+                nc.gpsimd.tensor_scalar(dst[:, v_end:g_end], src[:, v_end:g_end], 1.0, 0.0, MULT, ADD)
+            if g_end < P:
+                nc.scalar.copy(dst[:, g_end:P], src[:, g_end:P])
+            return wb
+
+        def quant_w(name, wb):
+            codes = [keep.tile([P, 2 * P], U32, name=f"{name}c{h}", align_bytes=64) for h in range(2)]
+            scales = [keep.tile([P, 2 * P], U8, name=f"{name}s{h}", align_bytes=64) for h in range(2)]
+            for h in range(2):
+                nc.vector.quantize_mx(codes[h][:].bitcast(FP8X4), scales[h][:], wb[:, 2 * h : 2 * h + 2].rearrange("p t m i -> p (t m i)"))
+            return codes, scales
+
+        wkb = round_w("wkb", wk_raw, 64, 64)
+        wkq = quant_w("wk", wkb)
+        xb_all = keep.tile([P, J, PACK], BF16, name="xb_all", tag="wk_raw", align_bytes=64)
+        xb = [xb_all[:, x_starts[c] : x_starts[c] + w, :] for c, w in enumerate(X_CHUNKS)]
+        for c, w in enumerate(X_CHUNKS):
+            nc.scalar.copy(xb[c][:, :, 0:2], g01[:, :, x_starts[c] : x_starts[c] + w].rearrange("p i j -> p j i"))
+        g23 = [keep.tile([P, 2, w], F32, name=f"g23_{c}") for c, w in enumerate(X_CHUNKS)]
+        for i in range(2, 4):
+            for c, w in enumerate(X_CHUNKS):
+                j0 = x_starts[c]
+                nc.vector.tensor_tensor(
+                    g23[c][:, i - 2, :], x_sb[i][:].indirect(offsets[:, j0 // 16 : (j0 + w) // 16]), wgt_sb[:, j0 : j0 + w], MULT
+                )
+        x_codes = [keep.tile([P, w], U32, name=f"xc{c}", align_bytes=64) for c, w in enumerate(X_CHUNKS)]
+        x_scales = [keep.tile([P, w], U8, name=f"xs{c}", align_bytes=64) for c, w in enumerate(X_CHUNKS)]
+
+        def finish_x(c):
+            nc.scalar.copy(xb[c][:, :, 2:4], g23[c][:].rearrange("p i j -> p j i"))
+
+        def quant_x(c):
+            nc.vector.quantize_mx(x_codes[c][:].bitcast(FP8X4), x_scales[c][:], xb[c].rearrange("p j i -> p (j i)"))
+
+        def product(tag, wq, u):
+            c, t0, rows = units[u]
+            w = CHUNKS[c]
+            xc = max(i for i in range(len(X_CHUNKS)) if x_starts[i] <= starts[c])
+            js = slice(starts[c] - x_starts[xc], starts[c] - x_starts[xc] + w)
+            bank = psum.tile([P, rows, w], F32, name=tag)
+            for r in range(rows):
+                t = t0 + r
+                cols = slice((t % 2) * P, (t % 2 + 1) * P)
+                nc.tensor.matmul_mx(
+                    bank[:, r, :], wq[0][t // 2][:, cols].bitcast(FP8X4), wq[1][t // 2][:, cols],
+                    x_codes[xc][:, js].bitcast(FP8X4), x_scales[xc][:, js], start=True, stop=True,
+                )
+            return bank
+
+
+        y = [keep.tile([P, PACK, w], F32, name=f"y{c}") for c, w in enumerate(CHUNKS)]
+        yb = [keep.tile([P, w, PACK], BF16, name=f"yb{c}", align_bytes=64) for c, w in enumerate(CHUNKS)]
+        y_scales = keep.tile([P, J], U8, name="y_scales", align_bytes=64)
+        words = out_1[0].rearrange("p j i -> p (j i)").bitcast(I32)
+        gates = {}
+
+        def gate(u):
+            c, t0, rows = units[u]
+            w = CHUNKS[c]
+            ke = product("ke", wkq, u)
+            gates[u] = keep.tile([P, rows, w], F32, name=f"gate{u}", tag=f"gate{SLOT[u]}")
+            nc.vector.tensor_tensor(gates[u][:], ke[:], st_of(u), MULT)
+            nc.scalar.activation(gates[u][:], gates[u][:], SILU)
+
+        SLOT = (0, 1, 2, 3, 4, 0, 2, 4)
+        ROUND_ON = "ggssv"
+
+        def finish(u, wvq):
+            c, t0, rows = units[u]
+            w = CHUNKS[c]
+            j0 = starts[c]
+            ve = product("ve", wvq, u)
+            nc.vector.tensor_tensor(y[c][:, t0 : t0 + rows, :], ve[:], gates[u][:], MULT)
+            nc.sync.dma_start(y_rows[:, t0 : t0 + rows, j0 : j0 + w], y[c][:, t0 : t0 + rows, :])
+            if t0 + rows == PACK:
+                if ROUND_ON[c] == "g":
+                    nc.gpsimd.tensor_scalar(yb[c][:], y[c][:].rearrange("p i j -> p j i"), 1.0, 0.0, MULT, ADD)
+                else:
+                    dst = yb[c][:].rearrange("p (a b) i -> p a i b", b=4)
+                    src = y[c][:].rearrange("p i (a b) -> p a i b", b=4)
+                    if ROUND_ON[c] == "s":
+                        nc.scalar.copy(dst, src)
+                    else:
+                        nc.vector.tensor_copy(dst, src)
+
+        def quant_y(c):
+            w = CHUNKS[c]
+            j0 = starts[c]
+            codes = keep.tile([P, w], U32, name=f"yc{c}", align_bytes=64)
+            nc.vector.quantize_mx(codes[:].bitcast(FP8X4), y_scales[:, j0 : j0 + w], yb[c][:].rearrange("p j i -> p (j i)"))
+            nc.sync.dma_start(words[:, j0 : j0 + w], codes[:].bitcast(I32))
+
+        finish_x(0)
+        finish_x(1)
+        quant_x(0)
+        quant_x(1)
+        finish_x(2)
+        wvb = round_w("wvb", wv_raw, 0, 0)
+        gate(0)
+        quant_x(2)
+        gate(1)
+        wvq = quant_w("wv", wvb)
+        gate(2)
+        finish_x(3)
+        gate(3)
+        quant_x(3)
+        gate(4)
+        finish(0, wvq)
+        finish(1, wvq)
+        gate(5)
+        finish(2, wvq)
+        quant_y(0)
+        finish(3, wvq)
+        gate(6)
+        finish(4, wvq)
+        finish(5, wvq)
+        gate(7)
+        quant_y(1)
+        finish(6, wvq)
+        quant_y(2)
+        finish(7, wvq)
+        quant_y(3)
+        quant_y(4)
+        for q in range(4):
+            nc.scalar.dma_start(out_2[0, 4 * q : 4 * q + 4, :].bitcast(I32), y_scales[32 * q : 32 * q + 4, :].bitcast(I32))

@@ -19,9 +19,15 @@ SILU = mybir.ActivationFunctionType.Silu
 P = 128
 PACK = 4
 BANK = 512
-X_CHUNKS = (256, 256, 256, 256)
+LIST = 16
+HALF = J // 2
+XW = 256
+
 CHUNKS = (256, 256, 256, 128, 128)
-ST_PIECES = ((0, 2, 0, 256), (2, 4, 0, 256), (0, 4, 256, 512), (0, 4, 512, 768), (0, 4, 768, 1024))
+ST_LOADS = ((0, 2, 0, 256), (2, 4, 0, 256), (0, 2, 256, 512), (2, 4, 256, 512), (0, 4, 512, 1024))
+GATE_BUFFER = (0, 1, 2, 3, 0, 1, 3, 0)
+WK_ON_VECTOR = 64
+WV_ON_VECTOR = 32
 
 
 def tile_list_siluP_kernel(tc, xT, wgt, wk, wv, st, offs, out_0, out_1, out_2):
@@ -31,10 +37,9 @@ def tile_list_siluP_kernel(tc, xT, wgt, wk, wv, st, offs, out_0, out_1, out_2):
         psum = ctx.enter_context(tc.psum_pool(name="psum", bufs=4))
 
         starts = [sum(CHUNKS[:c]) for c in range(len(CHUNKS))]
-        x_starts = [sum(X_CHUNKS[:c]) for c in range(len(X_CHUNKS))]
         units = []
-        for c, w in enumerate(CHUNKS):
-            rows = BANK // w
+        for c, width in enumerate(CHUNKS):
+            rows = BANK // width
             for t0 in range(0, PACK, rows):
                 units.append((c, t0, rows))
 
@@ -42,183 +47,185 @@ def tile_list_siluP_kernel(tc, xT, wgt, wk, wv, st, offs, out_0, out_1, out_2):
         nc.vector.memset(warm[:, 0:4], 0.0)
         nc.scalar.activation(warm[:, 4:8], warm[:, 0:4], SILU)
 
-        offsets = keep.tile([P, J // 16], U16, name="offsets")
-        nc.sync.dma_start(offsets[:], offs)
-        wgt_sb = keep.tile([P, J], F32, name="wgt_sb")
-        nc.sync.dma_start(wgt_sb[:], wgt)
         x_rows = xT.rearrange("(p i) t -> i p t", i=PACK)
-        x_sb = []
+        wk_rows = wk.rearrange("(p i) n -> p i n", i=PACK)
+        wv_rows = wv.rearrange("(p i) n -> p i n", i=PACK)
+        st_rows = st.rearrange("(p t) j -> p t j", t=PACK)
+        y_rows = out_0.rearrange("(p t) j -> p t j", t=PACK)
 
-        def load_x(i):
-            plane = keep.tile([P, T], F32, name=f"x{i}")
-            nc.sync.dma_start(plane[:], x_rows[i])
-            x_sb.append(plane)
+        def load(name, src, align_bytes=32):
+            tile = keep.tile(list(src.shape), F32, name=name, tag=name, align_bytes=align_bytes)
+            nc.sync.dma_start(tile[:], src)
+            return tile
 
-        st_rows = st.rearrange("(p i) j -> p i j", i=PACK)
-        y_rows = out_0.rearrange("(p i) j -> p i j", i=PACK)
-        st_sb = []
-
-        def load_w(name, w):
-            raw = keep.tile([P, PACK, N], F32, name=name, tag=name, align_bytes=64)
-            nc.sync.dma_start(raw[:], w.rearrange("(p i) n -> p i n", i=PACK))
-            return raw
-
-        def load_st(s):
-            t0, t1, j0, j1 = ST_PIECES[s]
-            piece = keep.tile([P, t1 - t0, j1 - j0], F32, name=f"st{s}")
-            nc.sync.dma_start(piece[:], st_rows[:, t0:t1, j0:j1])
-            st_sb.append(piece)
+        offsets = keep.tile([P, J // LIST], U16, name="offsets")
+        nc.sync.dma_start(offsets[:], offs)
+        wgt_sb = [load("wgt0", wgt[:, 0:HALF])]
+        x_sb = [load("x0", x_rows[0])]
+        wgt_sb.append(load("wgt1", wgt[:, HALF:J]))
+        for i in range(1, PACK):
+            x_sb.append(load(f"x{i}", x_rows[i]))
+        wk_cut = PACK * WK_ON_VECTOR
+        wk_first = load("wk_first", wk_rows[:, :, 0:wk_cut])
+        wk_second = load("wk_second", wk_rows[:, :, wk_cut:N])
+        wv_raw = load("wv_raw", wv_rows, align_bytes=64)
+        st_sb = [load(f"st{s}", st_rows[:, t0:t1, j0:j1]) for s, (t0, t1, j0, j1) in enumerate(ST_LOADS)]
 
         def st_of(u):
             c, t0, rows = units[u]
-            j0, w = starts[c], CHUNKS[c]
-            for s, (a, b, lo, hi) in enumerate(ST_PIECES):
-                if a <= t0 and t0 + rows <= b and lo <= j0 and j0 + w <= hi:
-                    return st_sb[s][:, t0 - a : t0 - a + rows, j0 - lo : j0 - lo + w]
+            j0, width = starts[c], CHUNKS[c]
+            for s, (first, end, lo, hi) in enumerate(ST_LOADS):
+                if first <= t0 and t0 + rows <= end and lo <= j0 and j0 + width <= hi:
+                    return st_sb[s][:, t0 - first : t0 - first + rows, j0 - lo : j0 - lo + width]
 
-        load_x(0)
-        load_x(1)
-        wk_raw = load_w("wk_raw", wk)
-        load_x(2)
-        load_x(3)
-        for s in range(0):
-            load_st(s)
-        wv_raw = load_w("wv_raw", wv)
-        for s in range(0, len(ST_PIECES)):
-            load_st(s)
+        def gather(dst, i, j0, width):
+            picks = offsets[:, j0 // LIST : (j0 + width) // LIST]
+            weights = wgt_sb[j0 // HALF][:, j0 % HALF : j0 % HALF + width]
+            nc.vector.tensor_tensor(dst, x_sb[i][:].indirect(picks), weights, MULT)
 
-        g01 = keep.tile([P, 2, J], F32, name="g01")
+        early01 = keep.tile([P, 2, HALF], F32, name="early01")
+        early23 = [keep.tile([P, 2, XW], F32, name=f"early23_{c}") for c in range(HALF // XW)]
+        late = keep.tile([P, PACK, HALF], F32, name="late")
         for i in range(2):
-            nc.vector.tensor_tensor(g01[:, i, :], x_sb[i][:].indirect(offsets[:]), wgt_sb[:], MULT)
-        def round_w(name, raw, v_end, g_end):
-            wb = keep.tile([P, PACK, P, PACK], BF16, name=name, align_bytes=64)
-            dst = wb[:].rearrange("p t m i -> p m i t")
-            src = raw[:].rearrange("p i (m t) -> p m i t", t=PACK)
-            if v_end > 0:
-                nc.vector.tensor_copy(dst[:, 0:v_end], src[:, 0:v_end])
-            if g_end > v_end:
-                nc.gpsimd.tensor_scalar(dst[:, v_end:g_end], src[:, v_end:g_end], 1.0, 0.0, MULT, ADD)
-            if g_end < P:
-                nc.scalar.copy(dst[:, g_end:P], src[:, g_end:P])
-            return wb
+            gather(early01[:, i, :], i, 0, HALF)
+            gather(late[:, i, :], i, HALF, HALF)
+        xb_early = keep.tile([P, HALF, PACK], BF16, name="xb_early", align_bytes=64)
+        nc.scalar.copy(xb_early[:, :, 0:2], early01[:].rearrange("p i j -> p j i"))
+        for i in range(2, PACK):
+            for c in range(HALF // XW):
+                gather(early23[c][:, i - 2, :], i, c * XW, XW)
+            gather(late[:, i, :], i, HALF, HALF)
 
-        def quant_w(name, wb):
-            codes = [keep.tile([P, 2 * P], U32, name=f"{name}c{h}", align_bytes=64) for h in range(2)]
-            scales = [keep.tile([P, 2 * P], U8, name=f"{name}s{h}", align_bytes=64) for h in range(2)]
-            for h in range(2):
-                nc.vector.quantize_mx(codes[h][:].bitcast(FP8X4), scales[h][:], wb[:, 2 * h : 2 * h + 2].rearrange("p t m i -> p (t m i)"))
+        x_codes = [keep.tile([P, XW], U32, name=f"x_codes{c}", align_bytes=64) for c in range(J // XW)]
+        x_scales = [keep.tile([P, XW], U8, name=f"x_scales{c}", align_bytes=64) for c in range(J // XW)]
+
+        def weave(copy, dst, src):
+            copy(dst.rearrange("p (a b) i -> p a i b", b=4), src.rearrange("p i (a b) -> p a i b", b=4))
+
+        def part(c):
+            return slice(c % 2 * XW, (c % 2 + 1) * XW)
+
+        def quantise(codes, scales, rounded):
+            nc.vector.quantize_mx(codes.bitcast(FP8X4), scales, rounded.rearrange("p c i -> p (c i)"))
+
+        def round_early_x(c):
+            nc.scalar.copy(xb_early[:, part(c), 2:PACK], early23[c][:].rearrange("p i j -> p j i"))
+
+        def dealt(rounded):
+            return rounded[:].rearrange("p t m i -> p m i t")
+
+        def by_m(raw):
+            return raw[:].rearrange("p i (m t) -> p m i t", t=PACK)
+
+        def quantise_w(name, rounded, calls):
+            codes = keep.tile([P, N], U32, name=f"{name}_codes", align_bytes=64)
+            scales = keep.tile([P, N], U8, name=f"{name}_scales", align_bytes=64)
+            rows = PACK // calls
+            for t0 in range(0, PACK, rows):
+                cols = slice(t0 * P, (t0 + rows) * P)
+                quantise(codes[:, cols], scales[:, cols], rounded[:, t0 : t0 + rows].rearrange("p t m i -> p (t m) i"))
             return codes, scales
 
-        wkb = round_w("wkb", wk_raw, 64, 64)
-        wkq = quant_w("wk", wkb)
-        xb_all = keep.tile([P, J, PACK], BF16, name="xb_all", tag="wk_raw", align_bytes=64)
-        xb = [xb_all[:, x_starts[c] : x_starts[c] + w, :] for c, w in enumerate(X_CHUNKS)]
-        for c, w in enumerate(X_CHUNKS):
-            nc.scalar.copy(xb[c][:, :, 0:2], g01[:, :, x_starts[c] : x_starts[c] + w].rearrange("p i j -> p j i"))
-        g23 = [keep.tile([P, 2, w], F32, name=f"g23_{c}") for c, w in enumerate(X_CHUNKS)]
-        for i in range(2, 4):
-            for c, w in enumerate(X_CHUNKS):
-                j0 = x_starts[c]
-                nc.vector.tensor_tensor(
-                    g23[c][:, i - 2, :], x_sb[i][:].indirect(offsets[:, j0 // 16 : (j0 + w) // 16]), wgt_sb[:, j0 : j0 + w], MULT
-                )
-        x_codes = [keep.tile([P, w], U32, name=f"xc{c}", align_bytes=64) for c, w in enumerate(X_CHUNKS)]
-        x_scales = [keep.tile([P, w], U8, name=f"xs{c}", align_bytes=64) for c, w in enumerate(X_CHUNKS)]
-
-        def finish_x(c):
-            nc.scalar.copy(xb[c][:, :, 2:4], g23[c][:].rearrange("p i j -> p j i"))
-
-        def quant_x(c):
-            nc.vector.quantize_mx(x_codes[c][:].bitcast(FP8X4), x_scales[c][:], xb[c].rearrange("p j i -> p (j i)"))
-
-        def product(tag, wq, u):
+        def product(tag, w_mx, u):
             c, t0, rows = units[u]
-            w = CHUNKS[c]
-            xc = max(i for i in range(len(X_CHUNKS)) if x_starts[i] <= starts[c])
-            js = slice(starts[c] - x_starts[xc], starts[c] - x_starts[xc] + w)
-            bank = psum.tile([P, rows, w], F32, name=tag)
+            width = CHUNKS[c]
+            xc = starts[c] // XW
+            places = slice(starts[c] % XW, starts[c] % XW + width)
+            bank = psum.tile([P, rows, width], F32, name=tag)
             for r in range(rows):
-                t = t0 + r
-                cols = slice((t % 2) * P, (t % 2 + 1) * P)
+                cols = slice((t0 + r) * P, (t0 + r + 1) * P)
                 nc.tensor.matmul_mx(
-                    bank[:, r, :], wq[0][t // 2][:, cols].bitcast(FP8X4), wq[1][t // 2][:, cols],
-                    x_codes[xc][:, js].bitcast(FP8X4), x_scales[xc][:, js], start=True, stop=True,
+                    bank[:, r, :],
+                    w_mx[0][:, cols].bitcast(FP8X4),
+                    w_mx[1][:, cols],
+                    x_codes[xc][:, places].bitcast(FP8X4),
+                    x_scales[xc][:, places],
+                    start=True,
+                    stop=True,
                 )
             return bank
 
-
-        y = [keep.tile([P, PACK, w], F32, name=f"y{c}") for c, w in enumerate(CHUNKS)]
-        yb = [keep.tile([P, w, PACK], BF16, name=f"yb{c}", align_bytes=64) for c, w in enumerate(CHUNKS)]
+        y = [keep.tile([P, PACK, width], F32, name=f"y{c}") for c, width in enumerate(CHUNKS)]
+        yb = [keep.tile([P, width, PACK], BF16, name=f"yb{c}", align_bytes=64) for c, width in enumerate(CHUNKS)]
         y_scales = keep.tile([P, J], U8, name="y_scales", align_bytes=64)
         words = out_1[0].rearrange("p j i -> p (j i)").bitcast(I32)
         gates = {}
 
         def gate(u):
             c, t0, rows = units[u]
-            w = CHUNKS[c]
-            ke = product("ke", wkq, u)
-            gates[u] = keep.tile([P, rows, w], F32, name=f"gate{u}", tag=f"gate{SLOT[u]}")
+            ke = product("ke", wk_mx, u)
+            gates[u] = keep.tile([P, rows, CHUNKS[c]], F32, name=f"gate{u}", tag=f"gate{GATE_BUFFER[u]}")
             nc.vector.tensor_tensor(gates[u][:], ke[:], st_of(u), MULT)
             nc.scalar.activation(gates[u][:], gates[u][:], SILU)
 
-        SLOT = (0, 1, 2, 3, 4, 0, 2, 4)
-        ROUND_ON = "ggssv"
-
-        def finish(u, wvq):
+        def finish(u):
             c, t0, rows = units[u]
-            w = CHUNKS[c]
-            j0 = starts[c]
-            ve = product("ve", wvq, u)
-            nc.vector.tensor_tensor(y[c][:, t0 : t0 + rows, :], ve[:], gates[u][:], MULT)
-            nc.sync.dma_start(y_rows[:, t0 : t0 + rows, j0 : j0 + w], y[c][:, t0 : t0 + rows, :])
-            if t0 + rows == PACK:
-                if ROUND_ON[c] == "g":
-                    nc.gpsimd.tensor_scalar(yb[c][:], y[c][:].rearrange("p i j -> p j i"), 1.0, 0.0, MULT, ADD)
-                else:
-                    dst = yb[c][:].rearrange("p (a b) i -> p a i b", b=4)
-                    src = y[c][:].rearrange("p i (a b) -> p a i b", b=4)
-                    if ROUND_ON[c] == "s":
-                        nc.scalar.copy(dst, src)
-                    else:
-                        nc.vector.tensor_copy(dst, src)
+            ve = product("ve", wv_mx, u)
+            result = y[c][:, t0 : t0 + rows, :]
+            nc.vector.tensor_tensor(result, ve[:], gates[u][:], MULT)
+            nc.sync.dma_start(y_rows[:, t0 : t0 + rows, starts[c] : starts[c] + CHUNKS[c]], result)
 
-        def quant_y(c):
-            w = CHUNKS[c]
-            j0 = starts[c]
-            codes = keep.tile([P, w], U32, name=f"yc{c}", align_bytes=64)
-            nc.vector.quantize_mx(codes[:].bitcast(FP8X4), y_scales[:, j0 : j0 + w], yb[c][:].rearrange("p j i -> p (j i)"))
-            nc.sync.dma_start(words[:, j0 : j0 + w], codes[:].bitcast(I32))
+        def round_y_on_gpsimd(c):
+            nc.gpsimd.tensor_scalar(yb[c][:], y[c][:].rearrange("p t j -> p j t"), 1.0, 0.0, MULT, ADD)
 
-        finish_x(0)
-        finish_x(1)
-        quant_x(0)
-        quant_x(1)
-        finish_x(2)
-        wvb = round_w("wvb", wv_raw, 0, 0)
+        def quantise_y(c):
+            places = slice(starts[c], starts[c] + CHUNKS[c])
+            codes = keep.tile([P, CHUNKS[c]], U32, name=f"y_codes{c}", align_bytes=64)
+            quantise(codes[:], y_scales[:, places], yb[c][:])
+            nc.sync.dma_start(words[:, places], codes[:].bitcast(I32))
+
+        wk_rounded = keep.tile([P, PACK, P, PACK], BF16, name="wk_rounded", align_bytes=64)
+        nc.vector.tensor_copy(dealt(wk_rounded)[:, 0:WK_ON_VECTOR], by_m(wk_first))
+        round_early_x(0)
+        round_early_x(1)
+        nc.scalar.copy(dealt(wk_rounded)[:, WK_ON_VECTOR:P], by_m(wk_second))
+        quantise(x_codes[0][:], x_scales[0][:], xb_early[:, part(0), :])
+        quantise(x_codes[1][:], x_scales[1][:], xb_early[:, part(1), :])
+        wk_mx = quantise_w("wk", wk_rounded, 2)
+
+        wv_rounded = keep.tile([P, PACK, P, PACK], BF16, name="wv_rounded", align_bytes=64)
+        nc.vector.tensor_copy(dealt(wv_rounded)[:, 0:WV_ON_VECTOR], by_m(wv_raw)[:, 0:WV_ON_VECTOR])
+        nc.scalar.copy(dealt(wv_rounded)[:, WV_ON_VECTOR:P], by_m(wv_raw)[:, WV_ON_VECTOR:P])
+        xb_late = keep.tile([P, HALF, PACK], BF16, name="xb_late", tag="wv_raw", align_bytes=64)
+
+        def round_late_x(c):
+            weave(nc.scalar.copy, xb_late[:, part(c), :], late[:, :, part(c)])
+
+        def quantise_late_x(c):
+            quantise(x_codes[c][:], x_scales[c][:], xb_late[:, part(c), :])
+
         gate(0)
-        quant_x(2)
         gate(1)
-        wvq = quant_w("wv", wvb)
+        round_late_x(2)
+        wv_mx = quantise_w("wv", wv_rounded, 1)
         gate(2)
-        finish_x(3)
         gate(3)
-        quant_x(3)
+        finish(0)
+        quantise_late_x(2)
+        finish(1)
+        round_y_on_gpsimd(0)
         gate(4)
-        finish(0, wvq)
-        finish(1, wvq)
+        round_late_x(3)
+        finish(2)
         gate(5)
-        finish(2, wvq)
-        quant_y(0)
-        finish(3, wvq)
+        quantise_late_x(3)
+        quantise_y(0)
+        finish(3)
+        round_y_on_gpsimd(1)
+        finish(4)
         gate(6)
-        finish(4, wvq)
-        finish(5, wvq)
         gate(7)
-        quant_y(1)
-        finish(6, wvq)
-        quant_y(2)
-        finish(7, wvq)
-        quant_y(3)
-        quant_y(4)
+        finish(5)
+        weave(nc.scalar.copy, yb[2][:], y[2][:])
+        quantise_y(1)
+        finish(6)
+        weave(nc.scalar.copy, yb[3][:], y[3][:])
+        finish(7)
+        quantise_y(2)
+        weave(nc.vector.tensor_copy, yb[4][:], y[4][:])
+        quantise_y(3)
+        quantise_y(4)
+
         for q in range(4):
-            nc.scalar.dma_start(out_2[0, 4 * q : 4 * q + 4, :].bitcast(I32), y_scales[32 * q : 32 * q + 4, :].bitcast(I32))
+            queue = nc.scalar if q < 2 else nc.sync
+            queue.dma_start(out_2[0, 4 * q : 4 * q + 4, :].bitcast(I32), y_scales[32 * q : 32 * q + 4, :].bitcast(I32))

from contextlib import ExitStack

import concourse.mybir as mybir

K, N, T, J = 512, 512, 2048, 1024
FLOPS = 2 * 2 * K * N * J

F32 = mybir.dt.float32
BF16 = mybir.dt.bfloat16
I32 = mybir.dt.int32
U32 = mybir.dt.uint32
U16 = mybir.dt.uint16
U8 = mybir.dt.uint8
FP8X4 = mybir.dt.float8_e4m3fn_x4
MULT = mybir.AluOpType.mult
ADD = mybir.AluOpType.add
SILU = mybir.ActivationFunctionType.Silu

P = 128
PACK = 4
BANK = 512
LIST = 16
HALF = J // 2
XW = 256

CHUNKS = (256, 256, 256, 128, 128)
ST_LOADS = ((0, 2, 0, 256), (2, 4, 0, 256), (0, 2, 256, 512), (2, 4, 256, 512), (0, 4, 512, 1024))
GATE_BUFFER = (0, 1, 2, 3, 0, 1, 3, 0)
WK_ON_VECTOR = 64
WV_ON_VECTOR = 32


def tile_list_siluP_kernel(tc, xT, wgt, wk, wv, st, offs, out_0, out_1, out_2):
    nc = tc.nc
    with ExitStack() as ctx:
        keep = ctx.enter_context(tc.tile_pool(name="keep", bufs=1))
        psum = ctx.enter_context(tc.psum_pool(name="psum", bufs=4))

        starts = [sum(CHUNKS[:c]) for c in range(len(CHUNKS))]
        units = []
        for c, width in enumerate(CHUNKS):
            rows = BANK // width
            for t0 in range(0, PACK, rows):
                units.append((c, t0, rows))

        warm = keep.tile([P, 8], F32, name="warm")
        nc.vector.memset(warm[:, 0:4], 0.0)
        nc.scalar.activation(warm[:, 4:8], warm[:, 0:4], SILU)

        x_rows = xT.rearrange("(p i) t -> i p t", i=PACK)
        wk_rows = wk.rearrange("(p i) n -> p i n", i=PACK)
        wv_rows = wv.rearrange("(p i) n -> p i n", i=PACK)
        st_rows = st.rearrange("(p t) j -> p t j", t=PACK)
        y_rows = out_0.rearrange("(p t) j -> p t j", t=PACK)

        def load(name, src, align_bytes=32):
            tile = keep.tile(list(src.shape), F32, name=name, tag=name, align_bytes=align_bytes)
            nc.sync.dma_start(tile[:], src)
            return tile

        offsets = keep.tile([P, J // LIST], U16, name="offsets")
        nc.sync.dma_start(offsets[:], offs)
        wgt_sb = [load("wgt0", wgt[:, 0:HALF])]
        x_sb = [load("x0", x_rows[0])]
        wgt_sb.append(load("wgt1", wgt[:, HALF:J]))
        for i in range(1, PACK):
            x_sb.append(load(f"x{i}", x_rows[i]))
        wk_cut = PACK * WK_ON_VECTOR
        wk_first = load("wk_first", wk_rows[:, :, 0:wk_cut])
        wk_second = load("wk_second", wk_rows[:, :, wk_cut:N])
        wv_raw = load("wv_raw", wv_rows, align_bytes=64)
        st_sb = [load(f"st{s}", st_rows[:, t0:t1, j0:j1]) for s, (t0, t1, j0, j1) in enumerate(ST_LOADS)]

        def st_of(u):
            c, t0, rows = units[u]
            j0, width = starts[c], CHUNKS[c]
            for s, (first, end, lo, hi) in enumerate(ST_LOADS):
                if first <= t0 and t0 + rows <= end and lo <= j0 and j0 + width <= hi:
                    return st_sb[s][:, t0 - first : t0 - first + rows, j0 - lo : j0 - lo + width]

        def gather(dst, i, j0, width):
            picks = offsets[:, j0 // LIST : (j0 + width) // LIST]
            weights = wgt_sb[j0 // HALF][:, j0 % HALF : j0 % HALF + width]
            nc.vector.tensor_tensor(dst, x_sb[i][:].indirect(picks), weights, MULT)

        early01 = keep.tile([P, 2, HALF], F32, name="early01")
        early23 = [keep.tile([P, 2, XW], F32, name=f"early23_{c}") for c in range(HALF // XW)]
        late = keep.tile([P, PACK, HALF], F32, name="late")
        for i in range(2):
            gather(early01[:, i, :], i, 0, HALF)
            gather(late[:, i, :], i, HALF, HALF)
        xb_early = keep.tile([P, HALF, PACK], BF16, name="xb_early", align_bytes=64)
        nc.scalar.copy(xb_early[:, :, 0:2], early01[:].rearrange("p i j -> p j i"))
        for i in range(2, PACK):
            for c in range(HALF // XW):
                gather(early23[c][:, i - 2, :], i, c * XW, XW)
            gather(late[:, i, :], i, HALF, HALF)

        x_codes = [keep.tile([P, XW], U32, name=f"x_codes{c}", align_bytes=64) for c in range(J // XW)]
        x_scales = [keep.tile([P, XW], U8, name=f"x_scales{c}", align_bytes=64) for c in range(J // XW)]

        def weave(copy, dst, src):
            copy(dst.rearrange("p (a b) i -> p a i b", b=4), src.rearrange("p i (a b) -> p a i b", b=4))

        def part(c):
            return slice(c % 2 * XW, (c % 2 + 1) * XW)

        def quantise(codes, scales, rounded):
            nc.vector.quantize_mx(codes.bitcast(FP8X4), scales, rounded.rearrange("p c i -> p (c i)"))

        def round_early_x(c):
            nc.scalar.copy(xb_early[:, part(c), 2:PACK], early23[c][:].rearrange("p i j -> p j i"))

        def dealt(rounded):
            return rounded[:].rearrange("p t m i -> p m i t")

        def by_m(raw):
            return raw[:].rearrange("p i (m t) -> p m i t", t=PACK)

        def quantise_w(name, rounded, calls):
            codes = keep.tile([P, N], U32, name=f"{name}_codes", align_bytes=64)
            scales = keep.tile([P, N], U8, name=f"{name}_scales", align_bytes=64)
            rows = PACK // calls
            for t0 in range(0, PACK, rows):
                cols = slice(t0 * P, (t0 + rows) * P)
                quantise(codes[:, cols], scales[:, cols], rounded[:, t0 : t0 + rows].rearrange("p t m i -> p (t m) i"))
            return codes, scales

        def product(tag, w_mx, u):
            c, t0, rows = units[u]
            width = CHUNKS[c]
            xc = starts[c] // XW
            places = slice(starts[c] % XW, starts[c] % XW + width)
            bank = psum.tile([P, rows, width], F32, name=tag)
            for r in range(rows):
                cols = slice((t0 + r) * P, (t0 + r + 1) * P)
                nc.tensor.matmul_mx(
                    bank[:, r, :],
                    w_mx[0][:, cols].bitcast(FP8X4),
                    w_mx[1][:, cols],
                    x_codes[xc][:, places].bitcast(FP8X4),
                    x_scales[xc][:, places],
                    start=True,
                    stop=True,
                )
            return bank

        y = [keep.tile([P, PACK, width], F32, name=f"y{c}") for c, width in enumerate(CHUNKS)]
        yb = [keep.tile([P, width, PACK], BF16, name=f"yb{c}", align_bytes=64) for c, width in enumerate(CHUNKS)]
        y_scales = keep.tile([P, J], U8, name="y_scales", align_bytes=64)
        words = out_1[0].rearrange("p j i -> p (j i)").bitcast(I32)
        gates = {}

        def gate(u):
            c, t0, rows = units[u]
            ke = product("ke", wk_mx, u)
            gates[u] = keep.tile([P, rows, CHUNKS[c]], F32, name=f"gate{u}", tag=f"gate{GATE_BUFFER[u]}")
            nc.vector.tensor_tensor(gates[u][:], ke[:], st_of(u), MULT)
            nc.scalar.activation(gates[u][:], gates[u][:], SILU)

        def finish(u):
            c, t0, rows = units[u]
            ve = product("ve", wv_mx, u)
            result = y[c][:, t0 : t0 + rows, :]
            nc.vector.tensor_tensor(result, ve[:], gates[u][:], MULT)
            nc.sync.dma_start(y_rows[:, t0 : t0 + rows, starts[c] : starts[c] + CHUNKS[c]], result)

        def round_y_on_gpsimd(c):
            nc.gpsimd.tensor_scalar(yb[c][:], y[c][:].rearrange("p t j -> p j t"), 1.0, 0.0, MULT, ADD)

        def quantise_y(c):
            places = slice(starts[c], starts[c] + CHUNKS[c])
            codes = keep.tile([P, CHUNKS[c]], U32, name=f"y_codes{c}", align_bytes=64)
            quantise(codes[:], y_scales[:, places], yb[c][:])
            nc.sync.dma_start(words[:, places], codes[:].bitcast(I32))

        wk_rounded = keep.tile([P, PACK, P, PACK], BF16, name="wk_rounded", align_bytes=64)
        nc.vector.tensor_copy(dealt(wk_rounded)[:, 0:WK_ON_VECTOR], by_m(wk_first))
        round_early_x(0)
        round_early_x(1)
        nc.scalar.copy(dealt(wk_rounded)[:, WK_ON_VECTOR:P], by_m(wk_second))
        quantise(x_codes[0][:], x_scales[0][:], xb_early[:, part(0), :])
        quantise(x_codes[1][:], x_scales[1][:], xb_early[:, part(1), :])
        wk_mx = quantise_w("wk", wk_rounded, 2)

        wv_rounded = keep.tile([P, PACK, P, PACK], BF16, name="wv_rounded", align_bytes=64)
        nc.vector.tensor_copy(dealt(wv_rounded)[:, 0:WV_ON_VECTOR], by_m(wv_raw)[:, 0:WV_ON_VECTOR])
        nc.scalar.copy(dealt(wv_rounded)[:, WV_ON_VECTOR:P], by_m(wv_raw)[:, WV_ON_VECTOR:P])
        xb_late = keep.tile([P, HALF, PACK], BF16, name="xb_late", tag="wv_raw", align_bytes=64)

        def round_late_x(c):
            weave(nc.scalar.copy, xb_late[:, part(c), :], late[:, :, part(c)])

        def quantise_late_x(c):
            quantise(x_codes[c][:], x_scales[c][:], xb_late[:, part(c), :])

        gate(0)
        gate(1)
        round_late_x(2)
        wv_mx = quantise_w("wv", wv_rounded, 1)
        gate(2)
        gate(3)
        finish(0)
        quantise_late_x(2)
        finish(1)
        round_y_on_gpsimd(0)
        gate(4)
        round_late_x(3)
        finish(2)
        gate(5)
        quantise_late_x(3)
        quantise_y(0)
        finish(3)
        round_y_on_gpsimd(1)
        finish(4)
        gate(6)
        gate(7)
        finish(5)
        weave(nc.scalar.copy, yb[2][:], y[2][:])
        quantise_y(1)
        finish(6)
        weave(nc.scalar.copy, yb[3][:], y[3][:])
        finish(7)
        quantise_y(2)
        weave(nc.vector.tensor_copy, yb[4][:], y[4][:])
        quantise_y(3)
        quantise_y(4)

        for q in range(4):
            queue = nc.scalar if q < 2 else nc.sync
            queue.dma_start(out_2[0, 4 * q : 4 * q + 4, :].bitcast(I32), y_scales[32 * q : 32 * q + 4, :].bitcast(I32))
